import numpy as np
import ml_dtypes


def mxq(x, axis, fmt="e4m3"):
    dtype, down = {"e4m3": (ml_dtypes.float8_e4m3fn, 7), "e5m2": (ml_dtypes.float8_e5m2, 14)}[fmt]
    v = np.moveaxis(np.asarray(x, np.float32).astype(ml_dtypes.bfloat16).astype(np.float64), axis, -1)
    blocks = v.reshape(v.shape[:-1] + (-1, 32))
    amax = np.abs(blocks).max(-1, keepdims=True)
    byte = np.maximum(np.where(amax > 0, np.frexp(amax)[1] - 1 + 127, 0) - down, 1)
    scale = np.exp2(byte - 127.0)
    codes = (blocks / scale).astype(np.float32).astype(dtype).astype(np.float64)
    return np.moveaxis((codes * scale).reshape(v.shape), -1, axis)


WIDE = False


def mx_kscale(k):
    if not WIDE:
        return np.ones(k)
    levels = np.array([10, -10, 5, -5, 0])
    if k % 512:
        return np.exp2(np.random.permutation(np.resize(levels, k // 32))).repeat(32)
    a = np.empty((k // 512, 16))
    for p in range(k // 512):
        a[p, :8] = np.random.permutation(np.resize(levels, 8))
        for g in range(8):
            far = levels[np.abs(levels - a[p, g]) >= 10]
            a[p, g + 8] = far[np.random.randint(len(far))]
    return np.exp2(a.ravel()).repeat(32)


def f64(x):
    return np.asarray(x).astype(np.float64)


def striped(idx):
    return np.tile(idx.reshape(-1, 16).T, (8, 1)).astype(np.uint16)


def unstriped(offs):
    return offs[:16].T.reshape(-1).astype(np.int64)


def gelu(v):
    return 0.5 * v * (1.0 + np.tanh(np.sqrt(2.0 / np.pi) * (v + 0.044715 * v**3)))


K, T, E, C, H, N = 512, 2048, 8, 256, 512, 256


def by_expert(wq, xq):
    return np.concatenate([wq[e].T @ xq[:, e * C:(e + 1) * C] for e in range(E)], axis=1)


def setup_inputs():
    n = np.random.standard_normal
    s = mx_kscale(K)[:, None]
    u = mx_kscale(H)
    return {
        "xT": (n((K, T)) * s).astype(np.float32),
        "w1": (n((E, K, H)) / np.sqrt(K) / s[None] * u[None, None, :]).astype(np.float32),
        "w2": (n((E, H, N)) / np.sqrt(H) / u[None, :, None]).astype(np.float32),
        "gate": np.tile(np.random.uniform(0.2, 1.0, E * C), (N, 1)).astype(np.float32),
        "offs": striped(np.random.permutation(T)[:E * C]),
    }


def reference(xT, w1, w2, gate, offs):
    idx = unstriped(offs)
    xq = mxq(f64(xT)[:, idx], 0, "e4m3")
    h = gelu(by_expert(mxq(f64(w1), 1, "e4m3"), xq))
    y = by_expert(mxq(f64(w2), 1, "e4m3"), mxq(h, 0, "e4m3"))
    out = np.zeros((N, T))
    out[:, idx] = f64(gate) * y
    return out

@@ -1,0 +1,240 @@
+from contextlib import ExitStack
+
+import concourse.mybir as mybir
+
+K, T, E, C, H, N = 512, 2048, 8, 256, 512, 256
+FLOPS = 2 * E * C * (K * H + H * N)
+
+F32 = mybir.dt.float32
+BF16 = mybir.dt.bfloat16
+U32 = mybir.dt.uint32
+U16 = mybir.dt.uint16
+U8 = mybir.dt.uint8
+FP8X4 = mybir.dt.float8_e4m3fn_x4
+GELU = mybir.ActivationFunctionType.Gelu_apprx_tanh
+MULT = mybir.AluOpType.mult
+ADD = mybir.AluOpType.add
+
+P = 128
+XC = 512
+GS = 1024
+LOADS_AHEAD = 3
+LATE = 2
+GROUPS = ((0, 1), (2, 3), (4, 5), (6,), (7,))
+G_W2 = (0, 1, 2)
+GATE_LATE = 2
+AHEAD = 3
+W_GROUPS = ((0, 1), (2, 3), (4, 5), (6,), (7,))
+
+
+def tile_routed_moe_kernel(tc, xT, w1, w2, gate, offs, out):
+    nc = tc.nc
+    with ExitStack() as ctx:
+        lists = ctx.enter_context(tc.tile_pool(name="lists", bufs=1))
+        keep = ctx.enter_context(tc.tile_pool(name="keep", bufs=1))
+        xraw_pool = ctx.enter_context(tc.tile_pool(name="xraw", bufs=4))
+        wraw_pool = ctx.enter_context(tc.tile_pool(name="wraw", bufs=4))
+        wgrp_pool = ctx.enter_context(tc.tile_pool(name="wgrp", bufs=3))
+        work = ctx.enter_context(tc.tile_pool(name="work", bufs=3))
+        psum_h = ctx.enter_context(tc.psum_pool(name="psum_h", bufs=5))
+        psum_y = ctx.enter_context(tc.psum_pool(name="psum_y", bufs=3))
+
+        offs_sb = lists.tile([P, E * C // 16], U16, name="offs_sb")
+        nc.sync.dma_start(offs_sb[:], offs)
+
+        warm_in = keep.tile([P, 1], F32, name="warm_in")
+        warm_out = keep.tile([P, 1], F32, name="warm_out")
+        nc.vector.memset(warm_in[:], 0.0)
+        nc.scalar.activation(out=warm_out[:], in_=warm_in[:], func=GELU)
+
+        x_view = xT.rearrange("(p j) n -> p j n", j=4)
+        pairs = [keep.tile([P, T, 2], BF16, name="pairs%d" % u) for u in range(2)]
+        for u in range(2):
+            for c in range(T // XC):
+                cols = slice(c * XC, (c + 1) * XC)
+                xraw = xraw_pool.tile([P, 2, XC], F32, name="xraw")
+                nc.sync.dma_start(xraw[:], x_view[:, 2 * u : 2 * u + 2, cols])
+                src = xraw[:].rearrange("p e (c i) -> p c e i", i=4)
+                dst = pairs[u][:, cols, :].rearrange("p (c i) e -> p c e i", i=4)
+                if u == 0:
+                    nc.vector.tensor_copy(out=dst, in_=src)
+                else:
+                    nc.scalar.copy(out=dst, in_=src)
+
+        w1raw, w2raw, gate_sb = {}, {}, {}
+        w1c, w1s, w2c, w2s = {}, {}, {}, {}
+        gate_view = gate.rearrange("(b p) s -> p b s", b=2)
+
+        def load_gate(g):
+            gate_sb[g] = keep.tile([P, 2, 2 * C], F32, name="gate%d" % g)
+            nc.sync.dma_start(gate_sb[g][:], gate_view[:, :, g * 2 * C : (g + 1) * 2 * C])
+
+        def load_w1(e):
+            w1raw[e] = wraw_pool.tile([P, 4, H], F32, name="w1raw")
+            nc.sync.dma_start(w1raw[e][:], w1[e].rearrange("(p j) c -> p j c", j=4))
+
+        def load_w2(e):
+            w2raw[e] = wraw_pool.tile([P, 4, N], F32, name="w2raw")
+            nc.sync.dma_start(w2raw[e][:], w2[e].rearrange("(p j) c -> p j c", j=4))
+
+        def load_w(e):
+            if e in w2raw or e >= E:
+                return
+            if e == E - 2:
+                load_w1(e)
+                load_w1(e + 1)
+                load_w2(e)
+                load_gate((e - GATE_LATE) // 2)
+                load_w2(e + 1)
+                load_gate(E // 2 - 1)
+                return
+            load_w1(e)
+            load_w2(e)
+            if e >= GATE_LATE and (e - GATE_LATE) % 2 == 0:
+                load_gate((e - GATE_LATE) // 2)
+
+        wgroup_of = {}
+        for wgrp in W_GROUPS:
+            for e in wgrp:
+                wgroup_of[e] = wgrp
+
+        def prep_w(e0):
+            if e0 >= E or wgroup_of[e0] in w1c:
+                return
+            wgrp = wgroup_of[e0]
+            n = len(wgrp)
+            w1g = wgrp_pool.tile([P, n * H * 4], BF16, name="w1g", align_bytes=64)
+            w2g = wgrp_pool.tile([P, n * N * 4], BF16, name="w2g", align_bytes=64)
+            for k, e in enumerate(wgrp):
+                load_w(e)
+                nc.scalar.copy(
+                    out=w1g[:, k * H * 4 : (k + 1) * H * 4].rearrange("p (t m j) -> p m j t", t=4, j=4),
+                    in_=w1raw[e][:].rearrange("p j (m t) -> p m j t", t=4),
+                )
+                w2dst = w2g[:, k * N * 4 : (k + 1) * N * 4]
+                if e in G_W2:
+                    nc.gpsimd.tensor_scalar(
+                        out=w2dst.rearrange("p (c j) -> p c j", j=4),
+                        in0=w2raw[e][:].rearrange("p j c -> p c j"),
+                        scalar1=1.0,
+                        scalar2=0.0,
+                        op0=MULT,
+                        op1=ADD,
+                    )
+                else:
+                    nc.scalar.copy(
+                        out=w2dst.rearrange("p (c i j) -> p c j i", i=4, j=4),
+                        in_=w2raw[e][:].rearrange("p j (c i) -> p c j i", i=4),
+                    )
+            w1c[wgrp] = keep.tile([P, n * H], U32, name="w1c%d" % wgrp[0], align_bytes=64)
+            w1s[wgrp] = keep.tile([P, n * H], U8, name="w1s%d" % wgrp[0], align_bytes=64)
+            nc.vector.quantize_mx(out=w1c[wgrp][:].bitcast(FP8X4), scales=w1s[wgrp][:], in_=w1g[:])
+            w2c[wgrp] = keep.tile([P, n * N], U32, name="w2c%d" % wgrp[0], align_bytes=64)
+            w2s[wgrp] = keep.tile([P, n * N], U8, name="w2s%d" % wgrp[0], align_bytes=64)
+            nc.vector.quantize_mx(out=w2c[wgrp][:].bitcast(FP8X4), scales=w2s[wgrp][:], in_=w2g[:])
+
+        n_chunks = E * C // GS
+        xg = [keep.tile([P, GS * 4], BF16, name="xg%d" % s, align_bytes=64) for s in range(n_chunks)]
+        xc = [keep.tile([P, GS], U32, name="xc%d" % s, align_bytes=64) for s in range(n_chunks)]
+        xs = [keep.tile([P, GS], U8, name="xs%d" % s, align_bytes=64) for s in range(n_chunks)]
+
+        def gather(u, s):
+            nc.vector.tensor_copy(
+                out=xg[s][:].bitcast(U32).rearrange("p (n u) -> p n u", u=2)[:, :, u],
+                in_=pairs[u][:]
+                .rearrange("p n e -> p (n e)")
+                .bitcast(U32)
+                .indirect(offs_sb[:, s * (GS // 16) : (s + 1) * (GS // 16)]),
+            )
+
+        def quantize_tokens(s):
+            nc.vector.quantize_mx(out=xc[s][:].bitcast(FP8X4), scales=xs[s][:], in_=xg[s][:])
+
+        win = [keep.tile([P, T], F32, name="win%d" % b) for b in range(2)]
+        hb, ysb = {}, {}
+        group_of = {}
+        for grp in GROUPS:
+            for e in grp:
+                group_of[e] = grp
+
+        def scatter(grp):
+            first, n = grp[0], len(grp) * C
+            for b in range(2):
+                nc.vector.tensor_tensor(
+                    out=win[b][:].indirect(offs_sb[:, first * (C // 16) : first * (C // 16) + n // 16]),
+                    in0=ysb[grp][:, b, :],
+                    in1=gate_sb[first // 2][:, b, (first % 2) * C : (first % 2) * C + n],
+                    op=MULT,
+                )
+
+        def layer1(e):
+            grp = group_of[e]
+            if e == grp[0]:
+                hb[grp] = work.tile([P, len(grp) * C * 4], BF16, name="hb", align_bytes=64, bufs=2)
+            wgrp = wgroup_of[e]
+            w0 = (e - wgrp[0]) * H
+            for half in range(2):
+                hp = psum_h.tile([P, 4, 128], F32, name="hp")
+                x0 = (e * C) % GS + half * 128
+                h0 = (e - grp[0]) * C + half * 128
+                for t in range(4):
+                    nc.tensor.matmul_mx(
+                        out=hp[:, t, :],
+                        lhsT=w1c[wgrp][:, w0 + t * 128 : w0 + (t + 1) * 128].bitcast(FP8X4),
+                        lhsT_scale=w1s[wgrp][:, w0 + t * 128 : w0 + (t + 1) * 128],
+                        rhs=xc[e * C // GS][:, x0 : x0 + 128].bitcast(FP8X4),
+                        rhs_scale=xs[e * C // GS][:, x0 : x0 + 128],
+                        start=True,
+                        stop=True,
+                    )
+                nc.scalar.activation(
+                    out=hb[grp][:, h0 * 4 : (h0 + 128) * 4].rearrange("p (n t) -> p n t", t=4),
+                    in_=hp[:].rearrange("p t n -> p n t"),
+                    func=GELU,
+                )
+
+        def layer2(grp):
+            n = len(grp) * C
+            hc = work.tile([P, n], U32, name="hc", align_bytes=64)
+            hs = work.tile([P, n], U8, name="hs", align_bytes=64)
+            nc.vector.quantize_mx(out=hc[:].bitcast(FP8X4), scales=hs[:], in_=hb[grp][:])
+            ysb[grp] = work.tile([P, 2, n], F32, name="ysb")
+            for k, e in enumerate(grp):
+                wgrp = wgroup_of[e]
+                w0 = (e - wgrp[0]) * N
+                yp = psum_y.tile([P, 2, C], F32, name="yp")
+                for b in range(2):
+                    nc.tensor.matmul_mx(
+                        out=yp[:, b, :],
+                        lhsT=w2c[wgrp][:, w0 + b * 128 : w0 + (b + 1) * 128].bitcast(FP8X4),
+                        lhsT_scale=w2s[wgrp][:, w0 + b * 128 : w0 + (b + 1) * 128],
+                        rhs=hc[:, k * C : (k + 1) * C].bitcast(FP8X4),
+                        rhs_scale=hs[:, k * C : (k + 1) * C],
+                        start=True,
+                        stop=True,
+                    )
+                nc.scalar.copy(out=ysb[grp][:, :, k * C : (k + 1) * C], in_=yp[:])
+
+        gather(0, 0)
+        gather(0, 1)
+        gather(1, 0)
+        quantize_tokens(0)
+        for i in range(E + LATE + 1):
+            if i < E:
+                for e in range(i + LOADS_AHEAD + 1):
+                    load_w(e)
+                prep_w(i)
+                layer1(i)
+                if i == group_of[i][-1]:
+                    layer2(group_of[i])
+                if i == 0:
+                    gather(1, 1)
+                    quantize_tokens(1)
+                for e in range(i + 1, i + AHEAD + 1):
+                    prep_w(e)
+            for grp in GROUPS:
+                if grp[-1] + LATE == i:
+                    scatter(grp)
+
+        for b in range(2):
+            nc.sync.dma_start(out[b * P : (b + 1) * P, :], win[b][:])

@@ -19,6 +19,8 @@ P = 128
 XC = 512
 GS = 1024
 LOADS_AHEAD = 3
+L2_LATE = 2
+RUN_AHEAD = 4
 LATE = 2
 GROUPS = ((0, 1), (2, 3), (4, 5), (6,), (7,))
 G_W2 = (0, 1, 2)
@@ -170,7 +172,7 @@ def tile_routed_moe_kernel(tc, xT, w1, w2, gate, offs, out):
         def layer1(e):
             grp = group_of[e]
             if e == grp[0]:
-                hb[grp] = work.tile([P, len(grp) * C * 4], BF16, name="hb", align_bytes=64, bufs=2)
+                hb[grp] = work.tile([P, len(grp) * C * 4], BF16, name="hb", align_bytes=64, bufs=3)
             wgrp = wgroup_of[e]
             w0 = (e - wgrp[0]) * H
             for half in range(2):
@@ -219,21 +221,22 @@ def tile_routed_moe_kernel(tc, xT, w1, w2, gate, offs, out):
         gather(0, 1)
         gather(1, 0)
         quantize_tokens(0)
-        for i in range(E + LATE + 1):
+        for i in range(E + L2_LATE + LATE + 1):
             if i < E:
                 for e in range(i + LOADS_AHEAD + 1):
                     load_w(e)
                 prep_w(i)
                 layer1(i)
-                if i == group_of[i][-1]:
-                    layer2(group_of[i])
                 if i == 0:
                     gather(1, 1)
                     quantize_tokens(1)
                 for e in range(i + 1, i + AHEAD + 1):
                     prep_w(e)
             for grp in GROUPS:
-                if grp[-1] + LATE == i:
+                if grp[-1] + (L2_LATE if grp[0] >= RUN_AHEAD else 0) == i:
+                    layer2(grp)
+            for grp in GROUPS:
+                if grp[-1] + (L2_LATE if grp[0] >= RUN_AHEAD else 0) + LATE == i:
                     scatter(grp)
 
         for b in range(2):

@@ -22,8 +22,8 @@ LOADS_AHEAD = 3
 L2_LATE = 2
 RUN_AHEAD = 4
 LATE = 2
-GROUPS = ((0, 1), (2, 3), (4, 5), (6,), (7,))
-G_W2 = (0, 1, 2)
+GROUPS = ((0,), (1,), (2, 3), (4, 5), (6,), (7,))
+G_W2 = (0, 1, 2, 3)
 GATE_LATE = 2
 AHEAD = 3
 W_GROUPS = ((0, 1), (2, 3), (4, 5), (6,), (7,))

@@ -23,7 +23,7 @@ L2_LATE = 2
 RUN_AHEAD = 4
 LATE = 2
 GROUPS = ((0,), (1,), (2, 3), (4, 5), (6,), (7,))
-G_W2 = (0, 1, 2, 3)
+G_W2 = (0, 1, 2, 3, 4)
 GATE_LATE = 2
 AHEAD = 3
 W_GROUPS = ((0, 1), (2, 3), (4, 5), (6,), (7,))

from contextlib import ExitStack

import concourse.mybir as mybir

K, T, E, C, H, N = 512, 2048, 8, 256, 512, 256
FLOPS = 2 * E * C * (K * H + H * N)

F32 = mybir.dt.float32
BF16 = mybir.dt.bfloat16
U32 = mybir.dt.uint32
U16 = mybir.dt.uint16
U8 = mybir.dt.uint8
FP8X4 = mybir.dt.float8_e4m3fn_x4
GELU = mybir.ActivationFunctionType.Gelu_apprx_tanh
MULT = mybir.AluOpType.mult
ADD = mybir.AluOpType.add

P = 128
XC = 512
GS = 1024
LOADS_AHEAD = 3
L2_LATE = 2
RUN_AHEAD = 4
LATE = 2
GROUPS = ((0,), (1,), (2, 3), (4, 5), (6,), (7,))
G_W2 = (0, 1, 2, 3, 4)
GATE_LATE = 2
AHEAD = 3
W_GROUPS = ((0, 1), (2, 3), (4, 5), (6,), (7,))


def tile_routed_moe_kernel(tc, xT, w1, w2, gate, offs, out):
    nc = tc.nc
    with ExitStack() as ctx:
        lists = ctx.enter_context(tc.tile_pool(name="lists", bufs=1))
        keep = ctx.enter_context(tc.tile_pool(name="keep", bufs=1))
        xraw_pool = ctx.enter_context(tc.tile_pool(name="xraw", bufs=4))
        wraw_pool = ctx.enter_context(tc.tile_pool(name="wraw", bufs=4))
        wgrp_pool = ctx.enter_context(tc.tile_pool(name="wgrp", bufs=3))
        work = ctx.enter_context(tc.tile_pool(name="work", bufs=3))
        psum_h = ctx.enter_context(tc.psum_pool(name="psum_h", bufs=5))
        psum_y = ctx.enter_context(tc.psum_pool(name="psum_y", bufs=3))

        offs_sb = lists.tile([P, E * C // 16], U16, name="offs_sb")
        nc.sync.dma_start(offs_sb[:], offs)

        warm_in = keep.tile([P, 1], F32, name="warm_in")
        warm_out = keep.tile([P, 1], F32, name="warm_out")
        nc.vector.memset(warm_in[:], 0.0)
        nc.scalar.activation(out=warm_out[:], in_=warm_in[:], func=GELU)

        x_view = xT.rearrange("(p j) n -> p j n", j=4)
        pairs = [keep.tile([P, T, 2], BF16, name="pairs%d" % u) for u in range(2)]
        for u in range(2):
            for c in range(T // XC):
                cols = slice(c * XC, (c + 1) * XC)
                xraw = xraw_pool.tile([P, 2, XC], F32, name="xraw")
                nc.sync.dma_start(xraw[:], x_view[:, 2 * u : 2 * u + 2, cols])
                src = xraw[:].rearrange("p e (c i) -> p c e i", i=4)
                dst = pairs[u][:, cols, :].rearrange("p (c i) e -> p c e i", i=4)
                if u == 0:
                    nc.vector.tensor_copy(out=dst, in_=src)
                else:
                    nc.scalar.copy(out=dst, in_=src)

        w1raw, w2raw, gate_sb = {}, {}, {}
        w1c, w1s, w2c, w2s = {}, {}, {}, {}
        gate_view = gate.rearrange("(b p) s -> p b s", b=2)

        def load_gate(g):
            gate_sb[g] = keep.tile([P, 2, 2 * C], F32, name="gate%d" % g)
            nc.sync.dma_start(gate_sb[g][:], gate_view[:, :, g * 2 * C : (g + 1) * 2 * C])

        def load_w1(e):
            w1raw[e] = wraw_pool.tile([P, 4, H], F32, name="w1raw")
            nc.sync.dma_start(w1raw[e][:], w1[e].rearrange("(p j) c -> p j c", j=4))

        def load_w2(e):
            w2raw[e] = wraw_pool.tile([P, 4, N], F32, name="w2raw")
            nc.sync.dma_start(w2raw[e][:], w2[e].rearrange("(p j) c -> p j c", j=4))

        def load_w(e):
            if e in w2raw or e >= E:
                return
            if e == E - 2:
                load_w1(e)
                load_w1(e + 1)
                load_w2(e)
                load_gate((e - GATE_LATE) // 2)
                load_w2(e + 1)
                load_gate(E // 2 - 1)
                return
            load_w1(e)
            load_w2(e)
            if e >= GATE_LATE and (e - GATE_LATE) % 2 == 0:
                load_gate((e - GATE_LATE) // 2)

        wgroup_of = {}
        for wgrp in W_GROUPS:
            for e in wgrp:
                wgroup_of[e] = wgrp

        def prep_w(e0):
            if e0 >= E or wgroup_of[e0] in w1c:
                return
            wgrp = wgroup_of[e0]
            n = len(wgrp)
            w1g = wgrp_pool.tile([P, n * H * 4], BF16, name="w1g", align_bytes=64)
            w2g = wgrp_pool.tile([P, n * N * 4], BF16, name="w2g", align_bytes=64)
            for k, e in enumerate(wgrp):
                load_w(e)
                nc.scalar.copy(
                    out=w1g[:, k * H * 4 : (k + 1) * H * 4].rearrange("p (t m j) -> p m j t", t=4, j=4),
                    in_=w1raw[e][:].rearrange("p j (m t) -> p m j t", t=4),
                )
                w2dst = w2g[:, k * N * 4 : (k + 1) * N * 4]
                if e in G_W2:
                    nc.gpsimd.tensor_scalar(
                        out=w2dst.rearrange("p (c j) -> p c j", j=4),
                        in0=w2raw[e][:].rearrange("p j c -> p c j"),
                        scalar1=1.0,
                        scalar2=0.0,
                        op0=MULT,
                        op1=ADD,
                    )
                else:
                    nc.scalar.copy(
                        out=w2dst.rearrange("p (c i j) -> p c j i", i=4, j=4),
                        in_=w2raw[e][:].rearrange("p j (c i) -> p c j i", i=4),
                    )
            w1c[wgrp] = keep.tile([P, n * H], U32, name="w1c%d" % wgrp[0], align_bytes=64)
            w1s[wgrp] = keep.tile([P, n * H], U8, name="w1s%d" % wgrp[0], align_bytes=64)
            nc.vector.quantize_mx(out=w1c[wgrp][:].bitcast(FP8X4), scales=w1s[wgrp][:], in_=w1g[:])
            w2c[wgrp] = keep.tile([P, n * N], U32, name="w2c%d" % wgrp[0], align_bytes=64)
            w2s[wgrp] = keep.tile([P, n * N], U8, name="w2s%d" % wgrp[0], align_bytes=64)
            nc.vector.quantize_mx(out=w2c[wgrp][:].bitcast(FP8X4), scales=w2s[wgrp][:], in_=w2g[:])

        n_chunks = E * C // GS
        xg = [keep.tile([P, GS * 4], BF16, name="xg%d" % s, align_bytes=64) for s in range(n_chunks)]
        xc = [keep.tile([P, GS], U32, name="xc%d" % s, align_bytes=64) for s in range(n_chunks)]
        xs = [keep.tile([P, GS], U8, name="xs%d" % s, align_bytes=64) for s in range(n_chunks)]

        def gather(u, s):
            nc.vector.tensor_copy(
                out=xg[s][:].bitcast(U32).rearrange("p (n u) -> p n u", u=2)[:, :, u],
                in_=pairs[u][:]
                .rearrange("p n e -> p (n e)")
                .bitcast(U32)
                .indirect(offs_sb[:, s * (GS // 16) : (s + 1) * (GS // 16)]),
            )

        def quantize_tokens(s):
            nc.vector.quantize_mx(out=xc[s][:].bitcast(FP8X4), scales=xs[s][:], in_=xg[s][:])

        win = [keep.tile([P, T], F32, name="win%d" % b) for b in range(2)]
        hb, ysb = {}, {}
        group_of = {}
        for grp in GROUPS:
            for e in grp:
                group_of[e] = grp

        def scatter(grp):
            first, n = grp[0], len(grp) * C
            for b in range(2):
                nc.vector.tensor_tensor(
                    out=win[b][:].indirect(offs_sb[:, first * (C // 16) : first * (C // 16) + n // 16]),
                    in0=ysb[grp][:, b, :],
                    in1=gate_sb[first // 2][:, b, (first % 2) * C : (first % 2) * C + n],
                    op=MULT,
                )

        def layer1(e):
            grp = group_of[e]
            if e == grp[0]:
                hb[grp] = work.tile([P, len(grp) * C * 4], BF16, name="hb", align_bytes=64, bufs=3)
            wgrp = wgroup_of[e]
            w0 = (e - wgrp[0]) * H
            for half in range(2):
                hp = psum_h.tile([P, 4, 128], F32, name="hp")
                x0 = (e * C) % GS + half * 128
                h0 = (e - grp[0]) * C + half * 128
                for t in range(4):
                    nc.tensor.matmul_mx(
                        out=hp[:, t, :],
                        lhsT=w1c[wgrp][:, w0 + t * 128 : w0 + (t + 1) * 128].bitcast(FP8X4),
                        lhsT_scale=w1s[wgrp][:, w0 + t * 128 : w0 + (t + 1) * 128],
                        rhs=xc[e * C // GS][:, x0 : x0 + 128].bitcast(FP8X4),
                        rhs_scale=xs[e * C // GS][:, x0 : x0 + 128],
                        start=True,
                        stop=True,
                    )
                nc.scalar.activation(
                    out=hb[grp][:, h0 * 4 : (h0 + 128) * 4].rearrange("p (n t) -> p n t", t=4),
                    in_=hp[:].rearrange("p t n -> p n t"),
                    func=GELU,
                )

        def layer2(grp):
            n = len(grp) * C
            hc = work.tile([P, n], U32, name="hc", align_bytes=64)
            hs = work.tile([P, n], U8, name="hs", align_bytes=64)
            nc.vector.quantize_mx(out=hc[:].bitcast(FP8X4), scales=hs[:], in_=hb[grp][:])
            ysb[grp] = work.tile([P, 2, n], F32, name="ysb")
            for k, e in enumerate(grp):
                wgrp = wgroup_of[e]
                w0 = (e - wgrp[0]) * N
                yp = psum_y.tile([P, 2, C], F32, name="yp")
                for b in range(2):
                    nc.tensor.matmul_mx(
                        out=yp[:, b, :],
                        lhsT=w2c[wgrp][:, w0 + b * 128 : w0 + (b + 1) * 128].bitcast(FP8X4),
                        lhsT_scale=w2s[wgrp][:, w0 + b * 128 : w0 + (b + 1) * 128],
                        rhs=hc[:, k * C : (k + 1) * C].bitcast(FP8X4),
                        rhs_scale=hs[:, k * C : (k + 1) * C],
                        start=True,
                        stop=True,
                    )
                nc.scalar.copy(out=ysb[grp][:, :, k * C : (k + 1) * C], in_=yp[:])

        gather(0, 0)
        gather(0, 1)
        gather(1, 0)
        quantize_tokens(0)
        for i in range(E + L2_LATE + LATE + 1):
            if i < E:
                for e in range(i + LOADS_AHEAD + 1):
                    load_w(e)
                prep_w(i)
                layer1(i)
                if i == 0:
                    gather(1, 1)
                    quantize_tokens(1)
                for e in range(i + 1, i + AHEAD + 1):
                    prep_w(e)
            for grp in GROUPS:
                if grp[-1] + (L2_LATE if grp[0] >= RUN_AHEAD else 0) == i:
                    layer2(grp)
            for grp in GROUPS:
                if grp[-1] + (L2_LATE if grp[0] >= RUN_AHEAD else 0) + LATE == i:
                    scatter(grp)

        for b in range(2):
            nc.sync.dma_start(out[b * P : (b + 1) * P, :], win[b][:])
